import numpy as np
import ml_dtypes


def mxq(x, axis, fmt="e4m3"):
    dtype, down = {"e4m3": (ml_dtypes.float8_e4m3fn, 7), "e5m2": (ml_dtypes.float8_e5m2, 14)}[fmt]
    v = np.moveaxis(np.asarray(x, np.float32).astype(ml_dtypes.bfloat16).astype(np.float64), axis, -1)
    blocks = v.reshape(v.shape[:-1] + (-1, 32))
    amax = np.abs(blocks).max(-1, keepdims=True)
    byte = np.maximum(np.where(amax > 0, np.frexp(amax)[1] - 1 + 127, 0) - down, 1)
    scale = np.exp2(byte - 127.0)
    codes = (blocks / scale).astype(np.float32).astype(dtype).astype(np.float64)
    return np.moveaxis((codes * scale).reshape(v.shape), -1, axis)


WIDE = False


def mx_kscale(k):
    if not WIDE:
        return np.ones(k)
    levels = np.array([10, -10, 5, -5, 0])
    if k % 512:
        return np.exp2(np.random.permutation(np.resize(levels, k // 32))).repeat(32)
    a = np.empty((k // 512, 16))
    for p in range(k // 512):
        a[p, :8] = np.random.permutation(np.resize(levels, 8))
        for g in range(8):
            far = levels[np.abs(levels - a[p, g]) >= 10]
            a[p, g + 8] = far[np.random.randint(len(far))]
    return np.exp2(a.ravel()).repeat(32)


def f64(x):
    return np.asarray(x).astype(np.float64)


def striped(idx):
    return np.tile(idx.reshape(-1, 16).T, (8, 1)).astype(np.uint16)


def unstriped(offs):
    return offs[:16].T.reshape(-1).astype(np.int64)


def striped8(idx):
    return np.concatenate([x.reshape(-1, 16).T for x in idx]).astype(np.uint16)


def runs(offs, k):
    lists = np.stack([offs[16 * r : 16 * r + 16].T.reshape(-1) for r in range(8)]).astype(np.int64)
    return lists[np.arange(k) % 512 // 64]


def pack_weight(w):
    k, n = w.shape
    w = f64(np.asarray(w, np.float32).astype(ml_dtypes.bfloat16)).reshape(k // 32, 32, n)
    amax = np.abs(w).max(1)
    byte = np.clip(np.where(amax > 0, np.frexp(amax)[1] - 1 + 127 - 7, 1), 1, 254)
    scaled = (w * np.exp2(127.0 - byte)[:, None, :]).reshape(k, n).astype(np.float32)
    words = np.ascontiguousarray(scaled.reshape(k // 512, 128, 4, n).transpose(0, 1, 3, 2)).astype(ml_dtypes.float8_e4m3fn).view(np.uint8)
    return words, np.ascontiguousarray(byte.astype(np.uint8).reshape(k // 512, 16, n))


def unpack_weight(words, scales):
    g, p, n, _ = words.shape
    vals = np.ascontiguousarray(words).view(ml_dtypes.float8_e4m3fn).astype(np.float64) * np.repeat(np.exp2(scales.astype(np.float64) - 127.0), 8, axis=1)[..., None]
    return vals.transpose(0, 1, 3, 2).reshape(g * 512, n)


K, T, S, N, G, H, W = 512, 1024, 512, 512, 2048, 512, 256


def setup_inputs():
    n = np.random.standard_normal
    s = mx_kscale(K)[:, None]
    u = mx_kscale(S)
    packed_xT = pack_weight(n((K, T)) * s)
    packed_dT = pack_weight(n((K, G)) / s)
    perm = np.stack([np.random.permutation(S) for _ in range(8)])
    return {
        "x_words": packed_xT[0],
        "x_scales": packed_xT[1],
        "d_words": packed_dT[0],
        "d_scales": packed_dT[1],
        "gn": (np.random.uniform(0.5, 1.5, (H, 1)) * u[:, None]).astype(np.float32),
        "gm": (np.random.uniform(0.5, 1.5, (H, 1)) * u[:, None]).astype(np.float32),
        "w1": (n((H, N)) / np.sqrt(2 * H) / u[:, None]).astype(np.float32),
        "w2": (n((H, N)) / np.sqrt(2 * H) / u[:, None]).astype(np.float32),
        "offs": striped(np.random.permutation(T)[:S]),
        "k1": striped8(np.random.randint(0, G, (8, H))),
        "two": striped(np.random.permutation(T)[:S]),
        "k2": striped8(np.random.randint(0, G, (8, H))),
        "n1": striped(np.random.permutation(S)),
        "n2": striped(np.random.permutation(S)),
        "n3": striped(np.random.permutation(S)),
        "n4": striped8(perm[:, :W]),
        "n5": striped8(perm[:, W:]),
        "n6": striped(np.random.permutation(S)),
        "n7": striped(np.random.permutation(S)),
    }


def reference(x_words, x_scales, d_words, d_scales, gn, gm, w1, w2, offs, k1, two, k2, n1, n2, n3, n4, n5, n6, n7):
    d_k1 = unpack_weight(d_words, d_scales)[np.arange(K)[:, None], runs(k1, K)]
    xq = unpack_weight(x_words, x_scales)[:, unstriped(offs)]
    a = 0.0625 * (d_k1.T @ xq)
    st = a - a[:, unstriped(n1)]
    su = np.maximum(st, st[:, unstriped(n2)])
    z = f64(gn) * (su + 0.5 * su[:, unstriped(n3)])
    d_k2 = unpack_weight(d_words, d_scales)[np.arange(K)[:, None], runs(k2, K)]
    x_two = unpack_weight(x_words, x_scales)[:, unstriped(two)]
    b = 0.0625 * (d_k2.T @ x_two)
    pb = b[np.arange(H)[:, None], runs(n5, H)]
    pa = b[np.arange(H)[:, None], runs(n4, H)]
    rb = pb - (0.5 * pa)
    ra = np.sqrt((pa) ** 2 + (pb) ** 2 + 0.25)
    ds = np.zeros((H, S))
    ds[np.arange(H)[:, None], runs(n4, H)] = ra
    dt = ds.copy()
    dt[np.arange(H)[:, None], runs(n5, H)] = rb
    z2 = f64(gm) * dt
    h = mxq(f64(w1), 0, "e4m3").T @ mxq(z, 0, "e4m3") + mxq(f64(w2), 0, "e4m3").T @ mxq(z2, 0, "e4m3")
    return h * (h[:, unstriped(n6)] - h[:, unstriped(n7)])

@@ -1,0 +1,243 @@
+from contextlib import ExitStack
+
+import concourse.mybir as mybir
+
+K, T, S, N, G, H, W = 512, 1024, 512, 512, 2048, 512, 256
+FLOPS = 4 * 2 * 512 * 512 * 512
+
+F32 = mybir.dt.float32
+BF16 = mybir.dt.bfloat16
+I32 = mybir.dt.int32
+U32 = mybir.dt.uint32
+U16 = mybir.dt.uint16
+U8 = mybir.dt.uint8
+FP8X4 = mybir.dt.float8_e4m3fn_x4
+ALU = mybir.AluOpType
+ACT = mybir.ActivationFunctionType
+
+P = 128
+PACK = 4
+HALF = S // 2
+LIST_HALF = HALF // 16
+
+
+def tile_picked_pqjthreepolarwind_none_p_kernel(
+    tc, x_words, x_scales, d_words, d_scales, gn, gm, w1, w2, offs, k1, two, k2, n1, n2, n3, n4, n5, n6, n7, out
+):
+    nc = tc.nc
+    with ExitStack() as ctx:
+        keep = ctx.enter_context(tc.tile_pool(name="keep", bufs=1))
+        psum = ctx.enter_context(tc.psum_pool(name="psum", bufs=1))
+
+        def tile(shape, dtype, name, tag=None):
+            return keep.tile(shape, dtype, name=name, tag=tag or name, align_bytes=64)
+
+        def load_list(src, name):
+            dst = keep.tile(list(src.shape), U16, name=name)
+            nc.sync.dma_start(dst[:], src)
+            return dst
+
+        def halves(lst):
+            return [(slice(h * HALF, (h + 1) * HALF), lst[:, h * LIST_HALF : (h + 1) * LIST_HALF]) for h in range(2)]
+
+        xw = tile([P, T], U32, "xw")
+        dw = tile([P, G], U32, "dw")
+        xs = tile([P, T], U8, "xs")
+        ds = tile([P, G], U8, "ds")
+        nc.vector.memset(ds[:].bitcast(I32), 0)
+        nc.gpsimd.memset(xs[:].bitcast(I32), 0)
+        quarter = tile([P, 1], F32, "quarter")
+        nc.gpsimd.memset(quarter[:], 0.25)
+
+        l_k2 = load_list(k2, "l_k2")
+        l_k1 = load_list(k1, "l_k1")
+        l_two = load_list(two, "l_two")
+        l_offs = load_list(offs, "l_offs")
+        l_n4 = load_list(n4, "l_n4")
+        nc.sync.dma_start(ds[0:P:8, :].bitcast(I32), d_scales[0].bitcast(I32))
+        nc.sync.dma_start(xs[0:P:8, :].bitcast(I32), x_scales[0].bitcast(I32))
+        w_parts = [[slice(0, N)], [slice(0, N // 2), slice(N // 2, N)]]
+        w_raw = [[tile([P, PACK, c.stop - c.start], F32, "w_raw%d%d" % (i, h)) for h, c in enumerate(w_parts[i])] for i in range(2)]
+
+        def load_w(i, h):
+            rows = (w2, w1)[i].rearrange("(p j) n -> p j n", j=PACK)
+            nc.sync.dma_start(w_raw[i][h][:], rows[:, :, w_parts[i][h]])
+
+        load_w(0, 0)
+        load_w(1, 0)
+        nc.sync.dma_start(xw[:].bitcast(I32), x_words[0].rearrange("p n t -> p (n t)").bitcast(I32))
+        nc.sync.dma_start(dw[:].bitcast(I32), d_words[0].rearrange("p n t -> p (n t)").bitcast(I32))
+        load_w(1, 1)
+        l_n5 = load_list(n5, "l_n5")
+
+        sc_g = tile([P, 2, H + S], U8, "sc_g")
+        sc = tile([P, 2, H + S], U8, "sc")
+        for i, (l_code, l_token) in enumerate(((l_k2, l_two), (l_k1, l_offs))):
+            nc.vector.tensor_copy(sc_g[:, i, :H], ds[:].indirect(l_code[:]))
+            nc.vector.tensor_copy(sc_g[:, i, H:], xs[:].indirect(l_token[:]))
+        nc.vector.tensor_copy(
+            sc[:, :, :H].rearrange("p i (t m) -> p i m t", t=PACK), sc_g[:, :, :H].rearrange("p i (m t) -> p i m t", t=PACK))
+        nc.vector.tensor_copy(sc[:, :, H:].bitcast(I32), sc_g[:, :, H:].bitcast(I32))
+        sc_rows = sc[:].rearrange("p i c -> p (i c)")
+        for r in range(1, 4):
+            nc.sync.dma_start(sc_rows[r:P:32, :].bitcast(I32), sc_rows[8 * r : P : 32, :].bitcast(I32))
+
+        l_n1 = load_list(n1, "l_n1")
+        l_n2 = load_list(n2, "l_n2")
+        l_n3 = load_list(n3, "l_n3")
+        l_n6 = load_list(n6, "l_n6")
+        l_n7 = load_list(n7, "l_n7")
+
+        def coded_product(i, l_code, l_token, name, tags):
+            xw_g = tile([P, S], U32, name + "_xw_g", tags[1])
+            nc.vector.tensor_copy(xw_g[:], xw[:].indirect(l_token[:]))
+            dw_g = tile([P, H], U32, name + "_dw_g", tags[2])
+            nc.vector.tensor_copy(dw_g[:], dw[:].indirect(l_code[:]))
+            dw_d = tile([P, H], U32, name + "_dw_d", tags[3])
+            nc.vector.tensor_copy(dw_d[:].rearrange("p (t m) -> p m t", t=PACK), dw_g[:].rearrange("p (m t) -> p m t", t=PACK))
+            banks = []
+            for t in range(PACK):
+                bank = psum.tile([P, S], F32, name="%s_bank%d" % (name, t), tag="%s%d" % (name, t))
+                cols = slice(t * P, (t + 1) * P)
+                nc.tensor.matmul_mx(out=bank[:], lhsT=dw_d[:, cols].bitcast(FP8X4), lhsT_scale=sc[:, i, cols],
+                                    rhs=xw_g[:].bitcast(FP8X4), rhs_scale=sc[:, i, H:], start=True, stop=True)
+                banks.append(bank)
+            return banks
+
+        def interleaved(dst):
+            return dst[:].rearrange("p (c i t) -> p c t i", i=4, t=PACK)
+
+        def planes(src):
+            return src[:].rearrange("p t (c i) -> p c t i", i=4)
+
+        def quantize(grouped, name, tag=None):
+            codes = tile([P, S], U32, name + "_codes", tag)
+            scales = tile([P, S], U8, name + "_scales")
+            nc.vector.quantize_mx(out=codes[:].bitcast(FP8X4), scales=scales[:], in_=grouped[:])
+            return codes, scales
+
+        b_banks = coded_product(0, l_k2, l_two, "b", ("", "slot1", "slot2", "slot3"))
+        a_banks = coded_product(1, l_k1, l_offs, "a", ("", "slot2", "slot3", "slot4"))
+
+        gm_sb = tile([P, PACK], F32, "gm_sb", "slot2")
+        nc.sync.dma_start(gm_sb[:], gm.rearrange("(p j) o -> p (j o)", j=PACK))
+        gn_sb = tile([P, PACK], F32, "gn_sb", "slot4")
+        nc.sync.dma_start(gn_sb[:], gn.rearrange("(p j) o -> p (j o)", j=PACK))
+        w_bf = [tile([P, N * PACK], BF16, "w_bf%d" % i) for i in range(2)]
+
+        def cast_w(i):
+            for h, c in enumerate(w_parts[i]):
+                half = w_bf[i][:, c.start * PACK : c.stop * PACK]
+                nc.scalar.copy(half.rearrange("p (c i t) -> p c t i", i=4, t=PACK), planes(w_raw[i][h]))
+
+        dts, ssums, sts, sus = [], [], [], []
+        z2_planes = tile([P, PACK, S], BF16, "z2_planes")
+        sg = tile([P, PACK, S], F32, "sg")
+        g3 = tile([P, PACK, S], F32, "g3")
+
+        def b_pairs(t):
+            b_sb = tile([P, S], F32, "b_sb%d" % t)
+            nc.scalar.activation(b_sb[:], b_banks[t][:], ACT.Copy, scale=0.0625)
+            pair = tile([P, 2 * W], F32, "pair%d" % t)
+            nc.scalar.activation(pair[:, :W], b_sb[:].indirect(l_n4[:]), ACT.Copy, scale=-0.5)
+            nc.scalar.activation(pair[:, W:], b_sb[:].indirect(l_n5[:]), ACT.Copy)
+            sq = tile([P, 2 * W], F32, "sq%d" % t)
+            nc.scalar.activation(sq[:], pair[:], ACT.Square)
+            dt = tile([P, S], F32, "dt%d" % t)
+            nc.vector.tensor_tensor(dt[:].indirect(l_n5[:]), pair[:, W:], pair[:, :W], ALU.add)
+            ssum = tile([P, W], F32, "ssum%d" % t)
+            nc.vector.scalar_tensor_tensor(ssum[:], sq[:, :W], 4.0, sq[:, W:], ALU.mult, ALU.add)
+            dts.append(dt)
+            ssums.append(ssum)
+
+        def b_root(t):
+            ra = tile([P, W], F32, "ra%d" % t)
+            nc.scalar.activation(ra[:], ssums[t][:], ACT.Sqrt, bias=quarter[:])
+            nc.vector.tensor_copy(dts[t][:].indirect(l_n4[:]), ra[:])
+
+        def b_gain(t):
+            if t < 2:
+                nc.scalar.activation(z2_planes[:, t, :], dts[t][:], ACT.Copy, scale=gm_sb[:, t : t + 1])
+            else:
+                nc.vector.tensor_scalar(z2_planes[:, t, :], dts[t][:], gm_sb[:, t : t + 1], None, ALU.mult)
+
+        def a_diff(t):
+            a_sb = tile([P, S], F32, "a_sb%d" % t)
+            nc.scalar.activation(a_sb[:], a_banks[t][:], ACT.Copy, scale=0.0625)
+            g1 = tile([P, S], F32, "g1_%d" % t)
+            for cols, part in halves(l_n1):
+                nc.scalar.activation(g1[:, cols], a_sb[:].indirect(part), ACT.Copy)
+            st = tile([P, S], F32, "st%d" % t)
+            nc.vector.scalar_tensor_tensor(st[:], a_banks[t][:], 0.0625, g1[:], ALU.mult, ALU.subtract)
+            sts.append(st)
+
+        def a_max(t):
+            g2 = tile([P, S], F32, "g2_%d" % t)
+            for cols, part in halves(l_n2):
+                nc.scalar.activation(g2[:, cols], sts[t][:].indirect(part), ACT.Copy)
+            su = tile([P, S], F32, "su%d" % t)
+            nc.vector.tensor_tensor(su[:], sts[t][:], g2[:], ALU.max)
+            sus.append(su)
+
+        def a_gain(t):
+            nc.vector.tensor_scalar(sg[:, t, :], sus[t][:], gn_sb[:, t : t + 1], None, ALU.mult)
+
+        cast_w(0)
+        cast_w(1)
+        for t in range(PACK):
+            b_pairs(t)
+        w_q = [quantize(w_bf[0], "w2", "slot1"), quantize(w_bf[1], "w1")]
+        for t in range(PACK):
+            a_diff(t)
+            b_root(t)
+        for t in range(PACK):
+            a_max(t)
+            a_gain(t)
+        for t in range(PACK):
+            b_gain(t)
+        z2_bf = tile([P, S * PACK], BF16, "z2_bf")
+        nc.vector.tensor_copy(interleaved(z2_bf), planes(z2_planes))
+        z2_q = quantize(z2_bf, "z2")
+
+        z_bf = tile([P, S * PACK], BF16, "z_bf")
+        z_codes = tile([P, S], U32, "z_codes")
+        z_scales = tile([P, S], U8, "z_scales")
+        for h, (cols, part) in enumerate(halves(l_n3)):
+            for t in range(PACK):
+                nc.scalar.activation(g3[:, t, cols], sg[:, t, :].indirect(part), ACT.Copy, scale=0.5)
+            wide = slice(h * HALF * PACK, (h + 1) * HALF * PACK)
+            nc.vector.tensor_tensor(
+                z_bf[:, wide].rearrange("p (c i t) -> p c t i", i=4, t=PACK),
+                sg[:, :, cols].rearrange("p t (c i) -> p c t i", i=4),
+                g3[:, :, cols].rearrange("p t (c i) -> p c t i", i=4),
+                ALU.add,
+            )
+            nc.vector.quantize_mx(out=z_codes[:, cols].bitcast(FP8X4), scales=z_scales[:, cols], in_=z_bf[:, wide])
+
+        h_banks = []
+        for m in range(N // P):
+            bank = psum.tile([P, S], F32, name="h_bank%d" % m, tag="b%d" % m)
+            cols = slice(m * P, (m + 1) * P)
+            nc.tensor.matmul_mx(out=bank[:], lhsT=w_q[0][0][:, cols].bitcast(FP8X4), lhsT_scale=w_q[0][1][:, cols],
+                                rhs=z2_q[0][:].bitcast(FP8X4), rhs_scale=z2_q[1][:], start=True, stop=False)
+            h_banks.append(bank)
+        for h in range(2):
+            part = slice(h * HALF, (h + 1) * HALF)
+            for m in range(N // P):
+                cols = slice(m * P, (m + 1) * P)
+                nc.tensor.matmul_mx(out=h_banks[m][:, part], lhsT=w_q[1][0][:, cols].bitcast(FP8X4), lhsT_scale=w_q[1][1][:, cols],
+                                    rhs=z_codes[:, part].bitcast(FP8X4), rhs_scale=z_scales[:, part], start=False, stop=(h == 1))
+        for m in range(N // P):
+            h_sb = tile([P, S], F32, "h_sb%d" % m)
+            nc.scalar.copy(h_sb[:], h_banks[m][:])
+            g7 = tile([P, S], F32, "g7_%d" % m)
+            diff = tile([P, S], F32, "diff%d" % m)
+            res = tile([P, S], F32, "res%d" % m)
+            for (cols, part6), (cols7, part7) in zip(halves(l_n6), halves(l_n7)):
+                nc.scalar.activation(g7[:, cols], h_sb[:].indirect(part7), ACT.Copy)
+                nc.vector.tensor_tensor(diff[:, cols], h_sb[:].indirect(part6), g7[:, cols], ALU.subtract)
+            pieces = 2 if m == N // P - 1 else 1
+            for c in range(pieces):
+                cols = slice(c * S // pieces, (c + 1) * S // pieces)
+                nc.vector.tensor_tensor(res[:, cols], diff[:, cols], h_sb[:, cols], ALU.mult)
+                nc.sync.dma_start(out[m * P : (m + 1) * P, cols], res[:, cols])

@@ -44,18 +44,19 @@ def tile_picked_pqjthreepolarwind_none_p_kernel(
         dw = tile([P, G], U32, "dw")
         xs = tile([P, T], U8, "xs")
         ds = tile([P, G], U8, "ds")
-        nc.vector.memset(ds[:].bitcast(I32), 0)
-        nc.gpsimd.memset(xs[:].bitcast(I32), 0)
+        nc.gpsimd.memset(ds[:].bitcast(I32), 0)
+        nc.vector.memset(xs[:].bitcast(I32), 0)
         quarter = tile([P, 1], F32, "quarter")
         nc.gpsimd.memset(quarter[:], 0.25)
 
+        warm = tile([P, 1], F32, "warm")
+        nc.scalar.activation(warm[:], quarter[:], ACT.Sqrt)
         l_k2 = load_list(k2, "l_k2")
+        nc.sync.dma_start(ds[0:P:8, :].bitcast(I32), d_scales[0].bitcast(I32))
         l_k1 = load_list(k1, "l_k1")
+        nc.sync.dma_start(xs[0:P:8, :].bitcast(I32), x_scales[0].bitcast(I32))
         l_two = load_list(two, "l_two")
         l_offs = load_list(offs, "l_offs")
-        l_n4 = load_list(n4, "l_n4")
-        nc.sync.dma_start(ds[0:P:8, :].bitcast(I32), d_scales[0].bitcast(I32))
-        nc.sync.dma_start(xs[0:P:8, :].bitcast(I32), x_scales[0].bitcast(I32))
         w_parts = [[slice(0, N)], [slice(0, N // 2), slice(N // 2, N)]]
         w_raw = [[tile([P, PACK, c.stop - c.start], F32, "w_raw%d%d" % (i, h)) for h, c in enumerate(w_parts[i])] for i in range(2)]
 
@@ -68,12 +69,14 @@ def tile_picked_pqjthreepolarwind_none_p_kernel(
         nc.sync.dma_start(xw[:].bitcast(I32), x_words[0].rearrange("p n t -> p (n t)").bitcast(I32))
         nc.sync.dma_start(dw[:].bitcast(I32), d_words[0].rearrange("p n t -> p (n t)").bitcast(I32))
         load_w(1, 1)
+        l_n4 = load_list(n4, "l_n4")
         l_n5 = load_list(n5, "l_n5")
 
         sc_g = tile([P, 2, H + S], U8, "sc_g")
         sc = tile([P, 2, H + S], U8, "sc")
-        for i, (l_code, l_token) in enumerate(((l_k2, l_two), (l_k1, l_offs))):
+        for i, l_code in enumerate((l_k2, l_k1)):
             nc.vector.tensor_copy(sc_g[:, i, :H], ds[:].indirect(l_code[:]))
+        for i, l_token in enumerate((l_two, l_offs)):
             nc.vector.tensor_copy(sc_g[:, i, H:], xs[:].indirect(l_token[:]))
         nc.vector.tensor_copy(
             sc[:, :, :H].rearrange("p i (t m) -> p i m t", t=PACK), sc_g[:, :, :H].rearrange("p i (m t) -> p i m t", t=PACK))
@@ -133,7 +136,6 @@ def tile_picked_pqjthreepolarwind_none_p_kernel(
         dts, ssums, sts, sus = [], [], [], []
         z2_planes = tile([P, PACK, S], BF16, "z2_planes")
         sg = tile([P, PACK, S], F32, "sg")
-        g3 = tile([P, PACK, S], F32, "g3")
 
         def b_pairs(t):
             b_sb = tile([P, S], F32, "b_sb%d" % t)
@@ -175,7 +177,7 @@ def tile_picked_pqjthreepolarwind_none_p_kernel(
             g2 = tile([P, S], F32, "g2_%d" % t)
             for cols, part in halves(l_n2):
                 nc.scalar.activation(g2[:, cols], sts[t][:].indirect(part), ACT.Copy)
-            su = tile([P, S], F32, "su%d" % t)
+            su = tile([P, S], F32, "su%d" % t, "su%d" % t)
             nc.vector.tensor_tensor(su[:], sts[t][:], g2[:], ALU.max)
             sus.append(su)
 
@@ -195,21 +197,24 @@ def tile_picked_pqjthreepolarwind_none_p_kernel(
             a_gain(t)
         for t in range(PACK):
             b_gain(t)
-        z2_bf = tile([P, S * PACK], BF16, "z2_bf")
+        z2_bf = tile([P, S * PACK], BF16, "z2_bf", "su3")
         nc.vector.tensor_copy(interleaved(z2_bf), planes(z2_planes))
         z2_q = quantize(z2_bf, "z2")
 
         z_bf = tile([P, S * PACK], BF16, "z_bf")
         z_codes = tile([P, S], U32, "z_codes")
         z_scales = tile([P, S], U8, "z_scales")
-        for h, (cols, part) in enumerate(halves(l_n3)):
+        pieces = [slice(lo, hi) for lo, hi in ((0,128),(128,256),(256,384),(384,512))]
+        for cols in pieces:
+            part = l_n3[:, cols.start // 16 : cols.stop // 16]
+            g3 = tile([P, PACK, cols.stop - cols.start], F32, "g3_%d" % cols.start)
             for t in range(PACK):
-                nc.scalar.activation(g3[:, t, cols], sg[:, t, :].indirect(part), ACT.Copy, scale=0.5)
-            wide = slice(h * HALF * PACK, (h + 1) * HALF * PACK)
+                nc.scalar.activation(g3[:, t, :], sg[:, t, :].indirect(part), ACT.Copy, scale=0.5)
+            wide = slice(cols.start * PACK, cols.stop * PACK)
             nc.vector.tensor_tensor(
                 z_bf[:, wide].rearrange("p (c i t) -> p c t i", i=4, t=PACK),
                 sg[:, :, cols].rearrange("p t (c i) -> p c t i", i=4),
-                g3[:, :, cols].rearrange("p t (c i) -> p c t i", i=4),
+                g3[:].rearrange("p t (c i) -> p c t i", i=4),
                 ALU.add,
             )
             nc.vector.quantize_mx(out=z_codes[:, cols].bitcast(FP8X4), scales=z_scales[:, cols], in_=z_bf[:, wide])
@@ -221,23 +226,32 @@ def tile_picked_pqjthreepolarwind_none_p_kernel(
             nc.tensor.matmul_mx(out=bank[:], lhsT=w_q[0][0][:, cols].bitcast(FP8X4), lhsT_scale=w_q[0][1][:, cols],
                                 rhs=z2_q[0][:].bitcast(FP8X4), rhs_scale=z2_q[1][:], start=True, stop=False)
             h_banks.append(bank)
-        for h in range(2):
-            part = slice(h * HALF, (h + 1) * HALF)
+        for part in pieces:
             for m in range(N // P):
                 cols = slice(m * P, (m + 1) * P)
                 nc.tensor.matmul_mx(out=h_banks[m][:, part], lhsT=w_q[1][0][:, cols].bitcast(FP8X4), lhsT_scale=w_q[1][1][:, cols],
-                                    rhs=z_codes[:, part].bitcast(FP8X4), rhs_scale=z_scales[:, part], start=False, stop=(h == 1))
+                                    rhs=z_codes[:, part].bitcast(FP8X4), rhs_scale=z_scales[:, part], start=False, stop=(part.stop == S))
         for m in range(N // P):
-            h_sb = tile([P, S], F32, "h_sb%d" % m)
-            nc.scalar.copy(h_sb[:], h_banks[m][:])
+            h_sb = tile([P, S], F32, "h_sb%d" % m, "g7_%d" % (m - 2) if m >= 2 else None)
+            if m in (1,):
+                nc.vector.tensor_copy(h_sb[:], h_banks[m][:])
+            else:
+                nc.scalar.copy(h_sb[:], h_banks[m][:])
             g7 = tile([P, S], F32, "g7_%d" % m)
             diff = tile([P, S], F32, "diff%d" % m)
             res = tile([P, S], F32, "res%d" % m)
-            for (cols, part6), (cols7, part7) in zip(halves(l_n6), halves(l_n7)):
-                nc.scalar.activation(g7[:, cols], h_sb[:].indirect(part7), ACT.Copy)
-                nc.vector.tensor_tensor(diff[:, cols], h_sb[:].indirect(part6), g7[:, cols], ALU.subtract)
-            pieces = 2 if m == N // P - 1 else 1
-            for c in range(pieces):
-                cols = slice(c * S // pieces, (c + 1) * S // pieces)
+            if m in (3,):
+                g6 = tile([P, S], F32, "g6_%d" % m)
+                for (cols, part6), (cols7, part7) in zip(halves(l_n6), halves(l_n7)):
+                    nc.scalar.activation(g7[:, cols], h_sb[:].indirect(part7), ACT.Copy)
+                    nc.scalar.activation(g6[:, cols], h_sb[:].indirect(part6), ACT.Copy)
+                    nc.vector.tensor_tensor(diff[:, cols], g6[:, cols], g7[:, cols], ALU.subtract)
+            else:
+                for (cols, part6), (cols7, part7) in zip(halves(l_n6), halves(l_n7)):
+                    nc.scalar.activation(g7[:, cols], h_sb[:].indirect(part7), ACT.Copy)
+                    nc.vector.tensor_tensor(diff[:, cols], h_sb[:].indirect(part6), g7[:, cols], ALU.subtract)
+            stores = 2 if m == N // P - 1 else 1
+            for c in range(stores):
+                cols = slice(c * S // stores, (c + 1) * S // stores)
                 nc.vector.tensor_tensor(res[:, cols], diff[:, cols], h_sb[:, cols], ALU.mult)
                 nc.sync.dma_start(out[m * P : (m + 1) * P, cols], res[:, cols])

@@ -65,9 +65,9 @@ def tile_picked_pqjthreepolarwind_none_p_kernel(
             nc.sync.dma_start(w_raw[i][h][:], rows[:, :, w_parts[i][h]])
 
         load_w(0, 0)
-        load_w(1, 0)
         nc.sync.dma_start(xw[:].bitcast(I32), x_words[0].rearrange("p n t -> p (n t)").bitcast(I32))
         nc.sync.dma_start(dw[:].bitcast(I32), d_words[0].rearrange("p n t -> p (n t)").bitcast(I32))
+        load_w(1, 0)
         load_w(1, 1)
         l_n4 = load_list(n4, "l_n4")
         l_n5 = load_list(n5, "l_n5")
@@ -79,7 +79,8 @@ def tile_picked_pqjthreepolarwind_none_p_kernel(
         for i, l_token in enumerate((l_two, l_offs)):
             nc.vector.tensor_copy(sc_g[:, i, H:], xs[:].indirect(l_token[:]))
         nc.vector.tensor_copy(
-            sc[:, :, :H].rearrange("p i (t m) -> p i m t", t=PACK), sc_g[:, :, :H].rearrange("p i (m t) -> p i m t", t=PACK))
+            sc[:, :, :H].rearrange("p l (t b i) -> p l b t i", t=PACK, i=16),
+            sc_g[:, :, :H].rearrange("p l (b i t) -> p l b t i", t=PACK, i=16))
         nc.vector.tensor_copy(sc[:, :, H:].bitcast(I32), sc_g[:, :, H:].bitcast(I32))
         sc_rows = sc[:].rearrange("p i c -> p (i c)")
         for r in range(1, 4):
@@ -97,7 +98,7 @@ def tile_picked_pqjthreepolarwind_none_p_kernel(
             dw_g = tile([P, H], U32, name + "_dw_g", tags[2])
             nc.vector.tensor_copy(dw_g[:], dw[:].indirect(l_code[:]))
             dw_d = tile([P, H], U32, name + "_dw_d", tags[3])
-            nc.vector.tensor_copy(dw_d[:].rearrange("p (t m) -> p m t", t=PACK), dw_g[:].rearrange("p (m t) -> p m t", t=PACK))
+            nc.vector.tensor_copy(dw_d[:].rearrange("p (t b i) -> p b t i", t=PACK, i=4), dw_g[:].rearrange("p (b i t) -> p b t i", t=PACK, i=4))
             banks = []
             for t in range(PACK):
                 bank = psum.tile([P, S], F32, name="%s_bank%d" % (name, t), tag="%s%d" % (name, t))
@@ -197,7 +198,7 @@ def tile_picked_pqjthreepolarwind_none_p_kernel(
             a_gain(t)
         for t in range(PACK):
             b_gain(t)
-        z2_bf = tile([P, S * PACK], BF16, "z2_bf", "su3")
+        z2_bf = tile([P, S * PACK], BF16, "z2_bf", "su2")
         nc.vector.tensor_copy(interleaved(z2_bf), planes(z2_planes))
         z2_q = quantize(z2_bf, "z2")
 
@@ -207,7 +208,7 @@ def tile_picked_pqjthreepolarwind_none_p_kernel(
         pieces = [slice(lo, hi) for lo, hi in ((0,128),(128,256),(256,384),(384,512))]
         for cols in pieces:
             part = l_n3[:, cols.start // 16 : cols.stop // 16]
-            g3 = tile([P, PACK, cols.stop - cols.start], F32, "g3_%d" % cols.start)
+            g3 = tile([P, PACK, cols.stop - cols.start], F32, "g3_%d" % cols.start, (None, "st3", "g2_3", "su3")[cols.start // 128])
             for t in range(PACK):
                 nc.scalar.activation(g3[:, t, :], sg[:, t, :].indirect(part), ACT.Copy, scale=0.5)
             wide = slice(cols.start * PACK, cols.stop * PACK)
@@ -219,36 +220,45 @@ def tile_picked_pqjthreepolarwind_none_p_kernel(
             )
             nc.vector.quantize_mx(out=z_codes[:, cols].bitcast(FP8X4), scales=z_scales[:, cols], in_=z_bf[:, wide])
 
-        h_banks = []
-        for m in range(N // P):
-            bank = psum.tile([P, S], F32, name="h_bank%d" % m, tag="b%d" % m)
-            cols = slice(m * P, (m + 1) * P)
-            nc.tensor.matmul_mx(out=bank[:], lhsT=w_q[0][0][:, cols].bitcast(FP8X4), lhsT_scale=w_q[0][1][:, cols],
-                                rhs=z2_q[0][:].bitcast(FP8X4), rhs_scale=z2_q[1][:], start=True, stop=False)
-            h_banks.append(bank)
-        for part in pieces:
+        early, late = slice(0, pieces[-1].start), pieces[-1]
+        h_early = [psum.tile([P, early.stop], F32, name="h_early%d" % m, tag="b%d" % m) for m in range(N // P)]
+        h_late = [psum.tile([P, late.stop - late.start], F32, name="h_late%d" % m, tag="a%d" % m) for m in range(N // P)]
+
+        def h_pass(w_planes, z_planes, part, start, stop):
             for m in range(N // P):
                 cols = slice(m * P, (m + 1) * P)
-                nc.tensor.matmul_mx(out=h_banks[m][:, part], lhsT=w_q[1][0][:, cols].bitcast(FP8X4), lhsT_scale=w_q[1][1][:, cols],
-                                    rhs=z_codes[:, part].bitcast(FP8X4), rhs_scale=z_scales[:, part], start=False, stop=(part.stop == S))
-        for m in range(N // P):
-            h_sb = tile([P, S], F32, "h_sb%d" % m, "g7_%d" % (m - 2) if m >= 2 else None)
-            if m in (1,):
-                nc.vector.tensor_copy(h_sb[:], h_banks[m][:])
+                dst = h_late[m][:] if part == late else h_early[m][:, part]
+                nc.tensor.matmul_mx(out=dst, lhsT=w_planes[0][:, cols].bitcast(FP8X4), lhsT_scale=w_planes[1][:, cols],
+                                    rhs=z_planes[0][:, part].bitcast(FP8X4), rhs_scale=z_planes[1][:, part], start=start, stop=stop)
+
+        h_pass(w_q[0], z2_q, slice(0, HALF), True, False)
+        h_pass(w_q[0], z2_q, pieces[2], False, False)
+        h_pass(w_q[0], z2_q, late, True, False)
+        for part in pieces:
+            h_pass(w_q[1], (z_codes, z_scales), part, False, part.stop >= early.stop)
+
+        h_sbs = [tile([P, S], F32, "h_sb%d" % m) for m in range(N // P)]
+        def leave(eng, m, part):
+            bank = h_late[m] if part == late else h_early[m]
+            if eng == "v":
+                nc.vector.tensor_copy(h_sbs[m][:, part], bank[:])
             else:
-                nc.scalar.copy(h_sb[:], h_banks[m][:])
+                nc.scalar.copy(h_sbs[m][:, part], bank[:])
+
+        for eng, m, part in (("s", 0, early), ("s", 1, early), ("s", 2, early), ("v", 0, late), ("v", 1, late), ("v", 2, late), ("v", 3, early), ("v", 3, late)):
+            leave(eng, m, part)
+        for m in range(N // P):
+            h_sb = h_sbs[m]
             g7 = tile([P, S], F32, "g7_%d" % m)
+            g6 = tile([P, S], F32, "g6_%d" % m, "g1_%d" % m)
             diff = tile([P, S], F32, "diff%d" % m)
             res = tile([P, S], F32, "res%d" % m)
-            if m in (3,):
-                g6 = tile([P, S], F32, "g6_%d" % m)
-                for (cols, part6), (cols7, part7) in zip(halves(l_n6), halves(l_n7)):
-                    nc.scalar.activation(g7[:, cols], h_sb[:].indirect(part7), ACT.Copy)
+            for h, ((cols, part6), (cols7, part7)) in enumerate(zip(halves(l_n6), halves(l_n7))):
+                nc.scalar.activation(g7[:, cols], h_sb[:].indirect(part7), ACT.Copy)
+                if 2 * m + h >= 5:
                     nc.scalar.activation(g6[:, cols], h_sb[:].indirect(part6), ACT.Copy)
                     nc.vector.tensor_tensor(diff[:, cols], g6[:, cols], g7[:, cols], ALU.subtract)
-            else:
-                for (cols, part6), (cols7, part7) in zip(halves(l_n6), halves(l_n7)):
-                    nc.scalar.activation(g7[:, cols], h_sb[:].indirect(part7), ACT.Copy)
+                else:
                     nc.vector.tensor_tensor(diff[:, cols], h_sb[:].indirect(part6), g7[:, cols], ALU.subtract)
             stores = 2 if m == N // P - 1 else 1
             for c in range(stores):

@@ -3,7 +3,7 @@ from contextlib import ExitStack
 import concourse.mybir as mybir
 
 K, T, S, N, G, H, W = 512, 1024, 512, 512, 2048, 512, 256
-FLOPS = 4 * 2 * 512 * 512 * 512
+FLOPS = 2 * (2 * K * H * S) + 2 * (2 * H * N * S)
 
 F32 = mybir.dt.float32
 BF16 = mybir.dt.bfloat16
@@ -17,8 +17,19 @@ ACT = mybir.ActivationFunctionType
 
 P = 128
 PACK = 4
+LAST = PACK - 1
+QUADRANT = 32
+BLOCK_PARTITIONS = 8
+LIST_ROWS = 16
+LINE_BYTES = 16
 HALF = S // 2
-LIST_HALF = HALF // 16
+PIECE = 128
+A_SCALE = 0.0625
+
+A_BANKS_ON_VECTOR = 2
+DIFF_ON_GPSIMD = (1, 2)
+EARLY_BANKS_ON_SCALAR = 2
+FUSED_HALVES = 5
 
 
 def tile_picked_pqjthreepolarwind_none_p_kernel(
@@ -37,8 +48,10 @@ def tile_picked_pqjthreepolarwind_none_p_kernel(
             nc.sync.dma_start(dst[:], src)
             return dst
 
-        def halves(lst):
-            return [(slice(h * HALF, (h + 1) * HALF), lst[:, h * LIST_HALF : (h + 1) * LIST_HALF]) for h in range(2)]
+        def entries(lst, cols):
+            return lst[:, cols.start // LIST_ROWS : cols.stop // LIST_ROWS]
+
+        halves = [slice(0, HALF), slice(HALF, S)]
 
         xw = tile([P, T], U32, "xw")
         dw = tile([P, G], U32, "dw")
@@ -51,40 +64,50 @@ def tile_picked_pqjthreepolarwind_none_p_kernel(
 
         warm = tile([P, 1], F32, "warm")
         nc.scalar.activation(warm[:], quarter[:], ACT.Sqrt)
+
         l_k2 = load_list(k2, "l_k2")
-        nc.sync.dma_start(ds[0:P:8, :].bitcast(I32), d_scales[0].bitcast(I32))
+        nc.sync.dma_start(ds[0:P:BLOCK_PARTITIONS, :].bitcast(I32), d_scales[0].bitcast(I32))
         l_k1 = load_list(k1, "l_k1")
-        nc.sync.dma_start(xs[0:P:8, :].bitcast(I32), x_scales[0].bitcast(I32))
+        nc.sync.dma_start(xs[0:P:BLOCK_PARTITIONS, :].bitcast(I32), x_scales[0].bitcast(I32))
         l_two = load_list(two, "l_two")
         l_offs = load_list(offs, "l_offs")
+
+        weights = (w2, w1)
         w_parts = [[slice(0, N)], [slice(0, N // 2), slice(N // 2, N)]]
-        w_raw = [[tile([P, PACK, c.stop - c.start], F32, "w_raw%d%d" % (i, h)) for h, c in enumerate(w_parts[i])] for i in range(2)]
+        w_raw = [
+            [tile([P, PACK, cols.stop - cols.start], F32, "w_raw%d%d" % (i, j)) for j, cols in enumerate(parts)]
+            for i, parts in enumerate(w_parts)
+        ]
 
-        def load_w(i, h):
-            rows = (w2, w1)[i].rearrange("(p j) n -> p j n", j=PACK)
-            nc.sync.dma_start(w_raw[i][h][:], rows[:, :, w_parts[i][h]])
+        def load_weight(i):
+            rows = weights[i].rearrange("(p t) n -> p t n", t=PACK)
+            for raw, cols in zip(w_raw[i], w_parts[i]):
+                nc.sync.dma_start(raw[:], rows[:, :, cols])
 
-        load_w(0, 0)
+        load_weight(0)
         nc.sync.dma_start(xw[:].bitcast(I32), x_words[0].rearrange("p n t -> p (n t)").bitcast(I32))
         nc.sync.dma_start(dw[:].bitcast(I32), d_words[0].rearrange("p n t -> p (n t)").bitcast(I32))
-        load_w(1, 0)
-        load_w(1, 1)
+        load_weight(1)
         l_n4 = load_list(n4, "l_n4")
         l_n5 = load_list(n5, "l_n5")
 
-        sc_g = tile([P, 2, H + S], U8, "sc_g")
-        sc = tile([P, 2, H + S], U8, "sc")
+        picked_scales = tile([P, 2, H + S], U8, "picked_scales")
+        scales = tile([P, 2, H + S], U8, "scales")
         for i, l_code in enumerate((l_k2, l_k1)):
-            nc.vector.tensor_copy(sc_g[:, i, :H], ds[:].indirect(l_code[:]))
+            nc.vector.tensor_copy(picked_scales[:, i, :H], ds[:].indirect(l_code[:]))
         for i, l_token in enumerate((l_two, l_offs)):
-            nc.vector.tensor_copy(sc_g[:, i, H:], xs[:].indirect(l_token[:]))
+            nc.vector.tensor_copy(picked_scales[:, i, H:], xs[:].indirect(l_token[:]))
         nc.vector.tensor_copy(
-            sc[:, :, :H].rearrange("p l (t b i) -> p l b t i", t=PACK, i=16),
-            sc_g[:, :, :H].rearrange("p l (b i t) -> p l b t i", t=PACK, i=16))
-        nc.vector.tensor_copy(sc[:, :, H:].bitcast(I32), sc_g[:, :, H:].bitcast(I32))
-        sc_rows = sc[:].rearrange("p i c -> p (i c)")
-        for r in range(1, 4):
-            nc.sync.dma_start(sc_rows[r:P:32, :].bitcast(I32), sc_rows[8 * r : P : 32, :].bitcast(I32))
+            scales[:, :, :H].rearrange("p l (t b i) -> p l b t i", t=PACK, i=LINE_BYTES),
+            picked_scales[:, :, :H].rearrange("p l (b i t) -> p l b t i", t=PACK, i=LINE_BYTES),
+        )
+        nc.vector.tensor_copy(scales[:, :, H:].bitcast(I32), picked_scales[:, :, H:].bitcast(I32))
+        scale_rows = scales[:].rearrange("p l c -> p (l c)")
+        for r in range(1, QUADRANT // BLOCK_PARTITIONS):
+            nc.sync.dma_start(
+                scale_rows[r:P:QUADRANT, :].bitcast(I32),
+                scale_rows[BLOCK_PARTITIONS * r : P : QUADRANT, :].bitcast(I32),
+            )
 
         l_n1 = load_list(n1, "l_n1")
         l_n2 = load_list(n2, "l_n2")
@@ -92,176 +115,175 @@ def tile_picked_pqjthreepolarwind_none_p_kernel(
         l_n6 = load_list(n6, "l_n6")
         l_n7 = load_list(n7, "l_n7")
 
-        def coded_product(i, l_code, l_token, name, tags):
-            xw_g = tile([P, S], U32, name + "_xw_g", tags[1])
-            nc.vector.tensor_copy(xw_g[:], xw[:].indirect(l_token[:]))
-            dw_g = tile([P, H], U32, name + "_dw_g", tags[2])
-            nc.vector.tensor_copy(dw_g[:], dw[:].indirect(l_code[:]))
-            dw_d = tile([P, H], U32, name + "_dw_d", tags[3])
-            nc.vector.tensor_copy(dw_d[:].rearrange("p (t b i) -> p b t i", t=PACK, i=4), dw_g[:].rearrange("p (b i t) -> p b t i", t=PACK, i=4))
+        line_words = LINE_BYTES // 4
+
+        def coded_product(i, l_code, l_token, name, token_tag, code_tag, dealt_tag):
+            tokens = tile([P, S], U32, name + "_tokens", token_tag)
+            nc.vector.tensor_copy(tokens[:], xw[:].indirect(l_token[:]))
+            codes = tile([P, H], U32, name + "_codes", code_tag)
+            nc.vector.tensor_copy(codes[:], dw[:].indirect(l_code[:]))
+            dealt = tile([P, H], U32, name + "_dealt", dealt_tag)
+            nc.vector.tensor_copy(
+                dealt[:].rearrange("p (t b i) -> p b t i", t=PACK, i=line_words),
+                codes[:].rearrange("p (b i t) -> p b t i", t=PACK, i=line_words),
+            )
             banks = []
             for t in range(PACK):
                 bank = psum.tile([P, S], F32, name="%s_bank%d" % (name, t), tag="%s%d" % (name, t))
                 cols = slice(t * P, (t + 1) * P)
-                nc.tensor.matmul_mx(out=bank[:], lhsT=dw_d[:, cols].bitcast(FP8X4), lhsT_scale=sc[:, i, cols],
-                                    rhs=xw_g[:].bitcast(FP8X4), rhs_scale=sc[:, i, H:], start=True, stop=True)
+                nc.tensor.matmul_mx(
+                    out=bank[:],
+                    lhsT=dealt[:, cols].bitcast(FP8X4),
+                    lhsT_scale=scales[:, i, cols],
+                    rhs=tokens[:].bitcast(FP8X4),
+                    rhs_scale=scales[:, i, H:],
+                    start=True,
+                    stop=True,
+                )
                 banks.append(bank)
             return banks
 
-        def interleaved(dst):
-            return dst[:].rearrange("p (c i t) -> p c t i", i=4, t=PACK)
+        def side_by_side(dst):
+            return dst.rearrange("p (c i t) -> p c t i", i=line_words, t=PACK)
 
-        def planes(src):
-            return src[:].rearrange("p t (c i) -> p c t i", i=4)
+        def row_tiles(src):
+            return src.rearrange("p t (c i) -> p c t i", i=line_words)
 
-        def quantize(grouped, name, tag=None):
-            codes = tile([P, S], U32, name + "_codes", tag)
-            scales = tile([P, S], U8, name + "_scales")
-            nc.vector.quantize_mx(out=codes[:].bitcast(FP8X4), scales=scales[:], in_=grouped[:])
-            return codes, scales
+        def quantize(rounded, name, tag=None):
+            words = tile([P, S], U32, name + "_words", tag)
+            block_scales = tile([P, S], U8, name + "_scales")
+            nc.vector.quantize_mx(out=words[:].bitcast(FP8X4), scales=block_scales[:], in_=rounded[:])
+            return words, block_scales
 
-        b_banks = coded_product(0, l_k2, l_two, "b", ("", "slot1", "slot2", "slot3"))
-        a_banks = coded_product(1, l_k1, l_offs, "a", ("", "slot2", "slot3", "slot4"))
+        b_banks = coded_product(0, l_k2, l_two, "b", "words1", "words2", "words3")
+        a_banks = coded_product(1, l_k1, l_offs, "a", "words2", "words3", "words4")
 
-        gm_sb = tile([P, PACK], F32, "gm_sb", "slot2")
-        nc.sync.dma_start(gm_sb[:], gm.rearrange("(p j) o -> p (j o)", j=PACK))
-        gn_sb = tile([P, PACK], F32, "gn_sb", "slot4")
-        nc.sync.dma_start(gn_sb[:], gn.rearrange("(p j) o -> p (j o)", j=PACK))
-        w_bf = [tile([P, N * PACK], BF16, "w_bf%d" % i) for i in range(2)]
+        gm_sb = tile([P, PACK], F32, "gm_sb", "words2")
+        nc.sync.dma_start(gm_sb[:], gm.rearrange("(p t) o -> p (t o)", t=PACK))
+        gn_sb = tile([P, PACK], F32, "gn_sb", "words4")
+        nc.sync.dma_start(gn_sb[:], gn.rearrange("(p t) o -> p (t o)", t=PACK))
 
-        def cast_w(i):
-            for h, c in enumerate(w_parts[i]):
-                half = w_bf[i][:, c.start * PACK : c.stop * PACK]
-                nc.scalar.copy(half.rearrange("p (c i t) -> p c t i", i=4, t=PACK), planes(w_raw[i][h]))
+        w_bf = [tile([P, N * PACK], BF16, "w_bf%d" % i) for i in range(len(weights))]
+        z2_tiles = tile([P, PACK, S], BF16, "z2_tiles")
+        gained = tile([P, PACK, S], F32, "gained")
 
-        dts, ssums, sts, sus = [], [], [], []
-        z2_planes = tile([P, PACK, S], BF16, "z2_planes")
-        sg = tile([P, PACK, S], F32, "sg")
+        for rounded, raws, parts in zip(w_bf, w_raw, w_parts):
+            for raw, cols in zip(raws, parts):
+                nc.scalar.copy(side_by_side(rounded[:, cols.start * PACK : cols.stop * PACK]), row_tiles(raw[:]))
 
-        def b_pairs(t):
+        dts, square_sums = [], []
+        for t in range(PACK):
             b_sb = tile([P, S], F32, "b_sb%d" % t)
-            nc.scalar.activation(b_sb[:], b_banks[t][:], ACT.Copy, scale=0.0625)
+            nc.scalar.activation(b_sb[:], b_banks[t][:], ACT.Copy, scale=A_SCALE)
             pair = tile([P, 2 * W], F32, "pair%d" % t)
             nc.scalar.activation(pair[:, :W], b_sb[:].indirect(l_n4[:]), ACT.Copy, scale=-0.5)
             nc.scalar.activation(pair[:, W:], b_sb[:].indirect(l_n5[:]), ACT.Copy)
-            sq = tile([P, 2 * W], F32, "sq%d" % t)
-            nc.scalar.activation(sq[:], pair[:], ACT.Square)
+            squares = tile([P, 2 * W], F32, "squares%d" % t)
+            nc.scalar.activation(squares[:], pair[:], ACT.Square)
             dt = tile([P, S], F32, "dt%d" % t)
             nc.vector.tensor_tensor(dt[:].indirect(l_n5[:]), pair[:, W:], pair[:, :W], ALU.add)
-            ssum = tile([P, W], F32, "ssum%d" % t)
-            nc.vector.scalar_tensor_tensor(ssum[:], sq[:, :W], 4.0, sq[:, W:], ALU.mult, ALU.add)
+            square_sum = tile([P, W], F32, "square_sum%d" % t)
+            nc.vector.scalar_tensor_tensor(square_sum[:], squares[:, :W], 4.0, squares[:, W:], ALU.mult, ALU.add)
             dts.append(dt)
-            ssums.append(ssum)
+            square_sums.append(square_sum)
 
-        def b_root(t):
+        w2_q = quantize(w_bf[0], "w2", "words1")
+        w1_q = quantize(w_bf[1], "w1")
+
+        sts = []
+        for t in range(PACK):
+            a_sb = tile([P, S], F32, "a_sb%d" % t)
+            if t < A_BANKS_ON_VECTOR:
+                nc.vector.tensor_scalar(a_sb[:], a_banks[t][:], A_SCALE, None, ALU.mult)
+            else:
+                nc.scalar.activation(a_sb[:], a_banks[t][:], ACT.Copy, scale=A_SCALE)
+            a_n1 = tile([P, S], F32, "a_n1_%d" % t)
+            for cols in halves:
+                nc.scalar.activation(a_n1[:, cols], a_sb[:].indirect(entries(l_n1, cols)), ACT.Copy)
+            st = tile([P, S], F32, "st%d" % t)
+            if t in DIFF_ON_GPSIMD:
+                nc.gpsimd.tensor_tensor(st[:], a_sb[:], a_n1[:], ALU.subtract)
+            else:
+                nc.vector.scalar_tensor_tensor(st[:], a_banks[t][:], A_SCALE, a_n1[:], ALU.mult, ALU.subtract)
+            sts.append(st)
             ra = tile([P, W], F32, "ra%d" % t)
-            nc.scalar.activation(ra[:], ssums[t][:], ACT.Sqrt, bias=quarter[:])
+            nc.scalar.activation(ra[:], square_sums[t][:], ACT.Sqrt, bias=quarter[:])
             nc.vector.tensor_copy(dts[t][:].indirect(l_n4[:]), ra[:])
 
-        def b_gain(t):
-            if t < 2:
-                nc.scalar.activation(z2_planes[:, t, :], dts[t][:], ACT.Copy, scale=gm_sb[:, t : t + 1])
+        for t in range(PACK):
+            st_n2 = tile([P, S], F32, "st_n2_%d" % t)
+            for cols in halves:
+                nc.scalar.activation(st_n2[:, cols], sts[t][:].indirect(entries(l_n2, cols)), ACT.Copy)
+            su = tile([P, S], F32, "su%d" % t)
+            nc.vector.tensor_tensor(su[:], sts[t][:], st_n2[:], ALU.max)
+            nc.vector.tensor_scalar(gained[:, t, :], su[:], gn_sb[:, t : t + 1], None, ALU.mult)
+
+        for t in range(PACK):
+            gain = gm_sb[:, t : t + 1]
+            if t == LAST:
+                nc.scalar.activation(z2_tiles[:, t, :], dts[t][:], ACT.Copy, scale=gain)
             else:
-                nc.vector.tensor_scalar(z2_planes[:, t, :], dts[t][:], gm_sb[:, t : t + 1], None, ALU.mult)
-
-        def a_diff(t):
-            a_sb = tile([P, S], F32, "a_sb%d" % t)
-            nc.scalar.activation(a_sb[:], a_banks[t][:], ACT.Copy, scale=0.0625)
-            g1 = tile([P, S], F32, "g1_%d" % t)
-            for cols, part in halves(l_n1):
-                nc.scalar.activation(g1[:, cols], a_sb[:].indirect(part), ACT.Copy)
-            st = tile([P, S], F32, "st%d" % t)
-            nc.vector.scalar_tensor_tensor(st[:], a_banks[t][:], 0.0625, g1[:], ALU.mult, ALU.subtract)
-            sts.append(st)
-
-        def a_max(t):
-            g2 = tile([P, S], F32, "g2_%d" % t)
-            for cols, part in halves(l_n2):
-                nc.scalar.activation(g2[:, cols], sts[t][:].indirect(part), ACT.Copy)
-            su = tile([P, S], F32, "su%d" % t, "su%d" % t)
-            nc.vector.tensor_tensor(su[:], sts[t][:], g2[:], ALU.max)
-            sus.append(su)
-
-        def a_gain(t):
-            nc.vector.tensor_scalar(sg[:, t, :], sus[t][:], gn_sb[:, t : t + 1], None, ALU.mult)
-
-        cast_w(0)
-        cast_w(1)
-        for t in range(PACK):
-            b_pairs(t)
-        w_q = [quantize(w_bf[0], "w2", "slot1"), quantize(w_bf[1], "w1")]
-        for t in range(PACK):
-            a_diff(t)
-            b_root(t)
-        for t in range(PACK):
-            a_max(t)
-            a_gain(t)
-        for t in range(PACK):
-            b_gain(t)
-        z2_bf = tile([P, S * PACK], BF16, "z2_bf", "su2")
-        nc.vector.tensor_copy(interleaved(z2_bf), planes(z2_planes))
+                nc.gpsimd.tensor_scalar(z2_tiles[:, t, :], dts[t][:], gain, 0.0, ALU.mult, ALU.add)
+        z2_bf = tile([P, S * PACK], BF16, "z2_bf", "su%d" % (LAST - 1))
+        nc.vector.tensor_copy(side_by_side(z2_bf[:]), row_tiles(z2_tiles[:]))
         z2_q = quantize(z2_bf, "z2")
 
         z_bf = tile([P, S * PACK], BF16, "z_bf")
-        z_codes = tile([P, S], U32, "z_codes")
+        z_words = tile([P, S], U32, "z_words")
         z_scales = tile([P, S], U8, "z_scales")
-        pieces = [slice(lo, hi) for lo, hi in ((0,128),(128,256),(256,384),(384,512))]
-        for cols in pieces:
-            part = l_n3[:, cols.start // 16 : cols.stop // 16]
-            g3 = tile([P, PACK, cols.stop - cols.start], F32, "g3_%d" % cols.start, (None, "st3", "g2_3", "su3")[cols.start // 128])
+        pieces = [slice(lo, lo + PIECE) for lo in range(0, S, PIECE)]
+        piece_tags = [None, "st%d" % LAST, "st_n2_%d" % LAST, "su%d" % LAST]
+        for cols, tag in zip(pieces, piece_tags):
+            half_n3 = tile([P, PACK, PIECE], F32, "half_n3_%d" % cols.start, tag)
             for t in range(PACK):
-                nc.scalar.activation(g3[:, t, :], sg[:, t, :].indirect(part), ACT.Copy, scale=0.5)
-            wide = slice(cols.start * PACK, cols.stop * PACK)
-            nc.vector.tensor_tensor(
-                z_bf[:, wide].rearrange("p (c i t) -> p c t i", i=4, t=PACK),
-                sg[:, :, cols].rearrange("p t (c i) -> p c t i", i=4),
-                g3[:].rearrange("p t (c i) -> p c t i", i=4),
-                ALU.add,
-            )
-            nc.vector.quantize_mx(out=z_codes[:, cols].bitcast(FP8X4), scales=z_scales[:, cols], in_=z_bf[:, wide])
+                nc.scalar.activation(half_n3[:, t, :], gained[:, t, :].indirect(entries(l_n3, cols)), ACT.Copy, scale=0.5)
+            rounded = z_bf[:, cols.start * PACK : cols.stop * PACK]
+            nc.vector.tensor_tensor(side_by_side(rounded), row_tiles(gained[:, :, cols]), row_tiles(half_n3[:]), ALU.add)
+            nc.vector.quantize_mx(out=z_words[:, cols].bitcast(FP8X4), scales=z_scales[:, cols], in_=rounded)
 
         early, late = slice(0, pieces[-1].start), pieces[-1]
         h_early = [psum.tile([P, early.stop], F32, name="h_early%d" % m, tag="b%d" % m) for m in range(N // P)]
-        h_late = [psum.tile([P, late.stop - late.start], F32, name="h_late%d" % m, tag="a%d" % m) for m in range(N // P)]
+        h_late = [psum.tile([P, PIECE], F32, name="h_late%d" % m, tag="a%d" % m) for m in range(N // P)]
 
-        def h_pass(w_planes, z_planes, part, start, stop):
+        def h_pass(w_q, z_q, part, start, stop):
             for m in range(N // P):
                 cols = slice(m * P, (m + 1) * P)
-                dst = h_late[m][:] if part == late else h_early[m][:, part]
-                nc.tensor.matmul_mx(out=dst, lhsT=w_planes[0][:, cols].bitcast(FP8X4), lhsT_scale=w_planes[1][:, cols],
-                                    rhs=z_planes[0][:, part].bitcast(FP8X4), rhs_scale=z_planes[1][:, part], start=start, stop=stop)
+                nc.tensor.matmul_mx(
+                    out=h_late[m][:] if part == late else h_early[m][:, part],
+                    lhsT=w_q[0][:, cols].bitcast(FP8X4),
+                    lhsT_scale=w_q[1][:, cols],
+                    rhs=z_q[0][:, part].bitcast(FP8X4),
+                    rhs_scale=z_q[1][:, part],
+                    start=start,
+                    stop=stop,
+                )
 
-        h_pass(w_q[0], z2_q, slice(0, HALF), True, False)
-        h_pass(w_q[0], z2_q, pieces[2], False, False)
-        h_pass(w_q[0], z2_q, late, True, False)
+        h_pass(w2_q, z2_q, halves[0], True, False)
+        h_pass(w2_q, z2_q, slice(HALF, early.stop), False, False)
+        h_pass(w2_q, z2_q, late, True, False)
         for part in pieces:
-            h_pass(w_q[1], (z_codes, z_scales), part, False, part.stop >= early.stop)
+            h_pass(w1_q, (z_words, z_scales), part, False, part.stop >= early.stop)
 
         h_sbs = [tile([P, S], F32, "h_sb%d" % m) for m in range(N // P)]
-        def leave(eng, m, part):
-            bank = h_late[m] if part == late else h_early[m]
-            if eng == "v":
-                nc.vector.tensor_copy(h_sbs[m][:, part], bank[:])
-            else:
-                nc.scalar.copy(h_sbs[m][:, part], bank[:])
-
-        for eng, m, part in (("s", 0, early), ("s", 1, early), ("s", 2, early), ("v", 0, late), ("v", 1, late), ("v", 2, late), ("v", 3, early), ("v", 3, late)):
-            leave(eng, m, part)
+        for m in range(EARLY_BANKS_ON_SCALAR):
+            nc.scalar.copy(h_sbs[m][:, early], h_early[m][:])
         for m in range(N // P):
-            h_sb = h_sbs[m]
-            g7 = tile([P, S], F32, "g7_%d" % m)
-            g6 = tile([P, S], F32, "g6_%d" % m, "g1_%d" % m)
+            if m >= EARLY_BANKS_ON_SCALAR:
+                nc.vector.tensor_copy(h_sbs[m][:, early], h_early[m][:])
+            nc.vector.tensor_copy(h_sbs[m][:, late], h_late[m][:])
+
+        for m, h_sb in enumerate(h_sbs):
+            h_n7 = tile([P, S], F32, "h_n7_%d" % m)
             diff = tile([P, S], F32, "diff%d" % m)
             res = tile([P, S], F32, "res%d" % m)
-            for h, ((cols, part6), (cols7, part7)) in enumerate(zip(halves(l_n6), halves(l_n7))):
-                nc.scalar.activation(g7[:, cols], h_sb[:].indirect(part7), ACT.Copy)
-                if 2 * m + h >= 5:
-                    nc.scalar.activation(g6[:, cols], h_sb[:].indirect(part6), ACT.Copy)
-                    nc.vector.tensor_tensor(diff[:, cols], g6[:, cols], g7[:, cols], ALU.subtract)
-                else:
-                    nc.vector.tensor_tensor(diff[:, cols], h_sb[:].indirect(part6), g7[:, cols], ALU.subtract)
-            stores = 2 if m == N // P - 1 else 1
-            for c in range(stores):
-                cols = slice(c * S // stores, (c + 1) * S // stores)
+            for j, cols in enumerate(halves):
+                nc.scalar.activation(h_n7[:, cols], h_sb[:].indirect(entries(l_n7, cols)), ACT.Copy)
+                h_at_n6 = h_sb[:].indirect(entries(l_n6, cols))
+                if len(halves) * m + j >= FUSED_HALVES:
+                    h_n6 = tile([P, HALF], F32, "h_n6_%d%d" % (m, j))
+                    nc.scalar.activation(h_n6[:], h_at_n6, ACT.Copy)
+                    h_at_n6 = h_n6[:]
+                nc.vector.tensor_tensor(diff[:, cols], h_at_n6, h_n7[:, cols], ALU.subtract)
+            for cols in halves if m == len(h_sbs) - 1 else [slice(0, S)]:
                 nc.vector.tensor_tensor(res[:, cols], diff[:, cols], h_sb[:, cols], ALU.mult)
                 nc.sync.dma_start(out[m * P : (m + 1) * P, cols], res[:, cols])

from contextlib import ExitStack

import concourse.mybir as mybir

K, T, S, N, G, H, W = 512, 1024, 512, 512, 2048, 512, 256
FLOPS = 2 * (2 * K * H * S) + 2 * (2 * H * N * S)

F32 = mybir.dt.float32
BF16 = mybir.dt.bfloat16
I32 = mybir.dt.int32
U32 = mybir.dt.uint32
U16 = mybir.dt.uint16
U8 = mybir.dt.uint8
FP8X4 = mybir.dt.float8_e4m3fn_x4
ALU = mybir.AluOpType
ACT = mybir.ActivationFunctionType

P = 128
PACK = 4
LAST = PACK - 1
QUADRANT = 32
BLOCK_PARTITIONS = 8
LIST_ROWS = 16
LINE_BYTES = 16
HALF = S // 2
PIECE = 128
A_SCALE = 0.0625

A_BANKS_ON_VECTOR = 2
DIFF_ON_GPSIMD = (1, 2)
EARLY_BANKS_ON_SCALAR = 2
FUSED_HALVES = 5


def tile_picked_pqjthreepolarwind_none_p_kernel(
    tc, x_words, x_scales, d_words, d_scales, gn, gm, w1, w2, offs, k1, two, k2, n1, n2, n3, n4, n5, n6, n7, out
):
    nc = tc.nc
    with ExitStack() as ctx:
        keep = ctx.enter_context(tc.tile_pool(name="keep", bufs=1))
        psum = ctx.enter_context(tc.psum_pool(name="psum", bufs=1))

        def tile(shape, dtype, name, tag=None):
            return keep.tile(shape, dtype, name=name, tag=tag or name, align_bytes=64)

        def load_list(src, name):
            dst = keep.tile(list(src.shape), U16, name=name)
            nc.sync.dma_start(dst[:], src)
            return dst

        def entries(lst, cols):
            return lst[:, cols.start // LIST_ROWS : cols.stop // LIST_ROWS]

        halves = [slice(0, HALF), slice(HALF, S)]

        xw = tile([P, T], U32, "xw")
        dw = tile([P, G], U32, "dw")
        xs = tile([P, T], U8, "xs")
        ds = tile([P, G], U8, "ds")
        nc.gpsimd.memset(ds[:].bitcast(I32), 0)
        nc.vector.memset(xs[:].bitcast(I32), 0)
        quarter = tile([P, 1], F32, "quarter")
        nc.gpsimd.memset(quarter[:], 0.25)

        warm = tile([P, 1], F32, "warm")
        nc.scalar.activation(warm[:], quarter[:], ACT.Sqrt)

        l_k2 = load_list(k2, "l_k2")
        nc.sync.dma_start(ds[0:P:BLOCK_PARTITIONS, :].bitcast(I32), d_scales[0].bitcast(I32))
        l_k1 = load_list(k1, "l_k1")
        nc.sync.dma_start(xs[0:P:BLOCK_PARTITIONS, :].bitcast(I32), x_scales[0].bitcast(I32))
        l_two = load_list(two, "l_two")
        l_offs = load_list(offs, "l_offs")

        weights = (w2, w1)
        w_parts = [[slice(0, N)], [slice(0, N // 2), slice(N // 2, N)]]
        w_raw = [
            [tile([P, PACK, cols.stop - cols.start], F32, "w_raw%d%d" % (i, j)) for j, cols in enumerate(parts)]
            for i, parts in enumerate(w_parts)
        ]

        def load_weight(i):
            rows = weights[i].rearrange("(p t) n -> p t n", t=PACK)
            for raw, cols in zip(w_raw[i], w_parts[i]):
                nc.sync.dma_start(raw[:], rows[:, :, cols])

        load_weight(0)
        nc.sync.dma_start(xw[:].bitcast(I32), x_words[0].rearrange("p n t -> p (n t)").bitcast(I32))
        nc.sync.dma_start(dw[:].bitcast(I32), d_words[0].rearrange("p n t -> p (n t)").bitcast(I32))
        load_weight(1)
        l_n4 = load_list(n4, "l_n4")
        l_n5 = load_list(n5, "l_n5")

        picked_scales = tile([P, 2, H + S], U8, "picked_scales")
        scales = tile([P, 2, H + S], U8, "scales")
        for i, l_code in enumerate((l_k2, l_k1)):
            nc.vector.tensor_copy(picked_scales[:, i, :H], ds[:].indirect(l_code[:]))
        for i, l_token in enumerate((l_two, l_offs)):
            nc.vector.tensor_copy(picked_scales[:, i, H:], xs[:].indirect(l_token[:]))
        nc.vector.tensor_copy(
            scales[:, :, :H].rearrange("p l (t b i) -> p l b t i", t=PACK, i=LINE_BYTES),
            picked_scales[:, :, :H].rearrange("p l (b i t) -> p l b t i", t=PACK, i=LINE_BYTES),
        )
        nc.vector.tensor_copy(scales[:, :, H:].bitcast(I32), picked_scales[:, :, H:].bitcast(I32))
        scale_rows = scales[:].rearrange("p l c -> p (l c)")
        for r in range(1, QUADRANT // BLOCK_PARTITIONS):
            nc.sync.dma_start(
                scale_rows[r:P:QUADRANT, :].bitcast(I32),
                scale_rows[BLOCK_PARTITIONS * r : P : QUADRANT, :].bitcast(I32),
            )

        l_n1 = load_list(n1, "l_n1")
        l_n2 = load_list(n2, "l_n2")
        l_n3 = load_list(n3, "l_n3")
        l_n6 = load_list(n6, "l_n6")
        l_n7 = load_list(n7, "l_n7")

        line_words = LINE_BYTES // 4

        def coded_product(i, l_code, l_token, name, token_tag, code_tag, dealt_tag):
            tokens = tile([P, S], U32, name + "_tokens", token_tag)
            nc.vector.tensor_copy(tokens[:], xw[:].indirect(l_token[:]))
            codes = tile([P, H], U32, name + "_codes", code_tag)
            nc.vector.tensor_copy(codes[:], dw[:].indirect(l_code[:]))
            dealt = tile([P, H], U32, name + "_dealt", dealt_tag)
            nc.vector.tensor_copy(
                dealt[:].rearrange("p (t b i) -> p b t i", t=PACK, i=line_words),
                codes[:].rearrange("p (b i t) -> p b t i", t=PACK, i=line_words),
            )
            banks = []
            for t in range(PACK):
                bank = psum.tile([P, S], F32, name="%s_bank%d" % (name, t), tag="%s%d" % (name, t))
                cols = slice(t * P, (t + 1) * P)
                nc.tensor.matmul_mx(
                    out=bank[:],
                    lhsT=dealt[:, cols].bitcast(FP8X4),
                    lhsT_scale=scales[:, i, cols],
                    rhs=tokens[:].bitcast(FP8X4),
                    rhs_scale=scales[:, i, H:],
                    start=True,
                    stop=True,
                )
                banks.append(bank)
            return banks

        def side_by_side(dst):
            return dst.rearrange("p (c i t) -> p c t i", i=line_words, t=PACK)

        def row_tiles(src):
            return src.rearrange("p t (c i) -> p c t i", i=line_words)

        def quantize(rounded, name, tag=None):
            words = tile([P, S], U32, name + "_words", tag)
            block_scales = tile([P, S], U8, name + "_scales")
            nc.vector.quantize_mx(out=words[:].bitcast(FP8X4), scales=block_scales[:], in_=rounded[:])
            return words, block_scales

        b_banks = coded_product(0, l_k2, l_two, "b", "words1", "words2", "words3")
        a_banks = coded_product(1, l_k1, l_offs, "a", "words2", "words3", "words4")

        gm_sb = tile([P, PACK], F32, "gm_sb", "words2")
        nc.sync.dma_start(gm_sb[:], gm.rearrange("(p t) o -> p (t o)", t=PACK))
        gn_sb = tile([P, PACK], F32, "gn_sb", "words4")
        nc.sync.dma_start(gn_sb[:], gn.rearrange("(p t) o -> p (t o)", t=PACK))

        w_bf = [tile([P, N * PACK], BF16, "w_bf%d" % i) for i in range(len(weights))]
        z2_tiles = tile([P, PACK, S], BF16, "z2_tiles")
        gained = tile([P, PACK, S], F32, "gained")

        for rounded, raws, parts in zip(w_bf, w_raw, w_parts):
            for raw, cols in zip(raws, parts):
                nc.scalar.copy(side_by_side(rounded[:, cols.start * PACK : cols.stop * PACK]), row_tiles(raw[:]))

        dts, square_sums = [], []
        for t in range(PACK):
            b_sb = tile([P, S], F32, "b_sb%d" % t)
            nc.scalar.activation(b_sb[:], b_banks[t][:], ACT.Copy, scale=A_SCALE)
            pair = tile([P, 2 * W], F32, "pair%d" % t)
            nc.scalar.activation(pair[:, :W], b_sb[:].indirect(l_n4[:]), ACT.Copy, scale=-0.5)
            nc.scalar.activation(pair[:, W:], b_sb[:].indirect(l_n5[:]), ACT.Copy)
            squares = tile([P, 2 * W], F32, "squares%d" % t)
            nc.scalar.activation(squares[:], pair[:], ACT.Square)
            dt = tile([P, S], F32, "dt%d" % t)
            nc.vector.tensor_tensor(dt[:].indirect(l_n5[:]), pair[:, W:], pair[:, :W], ALU.add)
            square_sum = tile([P, W], F32, "square_sum%d" % t)
            nc.vector.scalar_tensor_tensor(square_sum[:], squares[:, :W], 4.0, squares[:, W:], ALU.mult, ALU.add)
            dts.append(dt)
            square_sums.append(square_sum)

        w2_q = quantize(w_bf[0], "w2", "words1")
        w1_q = quantize(w_bf[1], "w1")

        sts = []
        for t in range(PACK):
            a_sb = tile([P, S], F32, "a_sb%d" % t)
            if t < A_BANKS_ON_VECTOR:
                nc.vector.tensor_scalar(a_sb[:], a_banks[t][:], A_SCALE, None, ALU.mult)
            else:
                nc.scalar.activation(a_sb[:], a_banks[t][:], ACT.Copy, scale=A_SCALE)
            a_n1 = tile([P, S], F32, "a_n1_%d" % t)
            for cols in halves:
                nc.scalar.activation(a_n1[:, cols], a_sb[:].indirect(entries(l_n1, cols)), ACT.Copy)
            st = tile([P, S], F32, "st%d" % t)
            if t in DIFF_ON_GPSIMD:
                nc.gpsimd.tensor_tensor(st[:], a_sb[:], a_n1[:], ALU.subtract)
            else:
                nc.vector.scalar_tensor_tensor(st[:], a_banks[t][:], A_SCALE, a_n1[:], ALU.mult, ALU.subtract)
            sts.append(st)
            ra = tile([P, W], F32, "ra%d" % t)
            nc.scalar.activation(ra[:], square_sums[t][:], ACT.Sqrt, bias=quarter[:])
            nc.vector.tensor_copy(dts[t][:].indirect(l_n4[:]), ra[:])

        for t in range(PACK):
            st_n2 = tile([P, S], F32, "st_n2_%d" % t)
            for cols in halves:
                nc.scalar.activation(st_n2[:, cols], sts[t][:].indirect(entries(l_n2, cols)), ACT.Copy)
            su = tile([P, S], F32, "su%d" % t)
            nc.vector.tensor_tensor(su[:], sts[t][:], st_n2[:], ALU.max)
            nc.vector.tensor_scalar(gained[:, t, :], su[:], gn_sb[:, t : t + 1], None, ALU.mult)

        for t in range(PACK):
            gain = gm_sb[:, t : t + 1]
            if t == LAST:
                nc.scalar.activation(z2_tiles[:, t, :], dts[t][:], ACT.Copy, scale=gain)
            else:
                nc.gpsimd.tensor_scalar(z2_tiles[:, t, :], dts[t][:], gain, 0.0, ALU.mult, ALU.add)
        z2_bf = tile([P, S * PACK], BF16, "z2_bf", "su%d" % (LAST - 1))
        nc.vector.tensor_copy(side_by_side(z2_bf[:]), row_tiles(z2_tiles[:]))
        z2_q = quantize(z2_bf, "z2")

        z_bf = tile([P, S * PACK], BF16, "z_bf")
        z_words = tile([P, S], U32, "z_words")
        z_scales = tile([P, S], U8, "z_scales")
        pieces = [slice(lo, lo + PIECE) for lo in range(0, S, PIECE)]
        piece_tags = [None, "st%d" % LAST, "st_n2_%d" % LAST, "su%d" % LAST]
        for cols, tag in zip(pieces, piece_tags):
            half_n3 = tile([P, PACK, PIECE], F32, "half_n3_%d" % cols.start, tag)
            for t in range(PACK):
                nc.scalar.activation(half_n3[:, t, :], gained[:, t, :].indirect(entries(l_n3, cols)), ACT.Copy, scale=0.5)
            rounded = z_bf[:, cols.start * PACK : cols.stop * PACK]
            nc.vector.tensor_tensor(side_by_side(rounded), row_tiles(gained[:, :, cols]), row_tiles(half_n3[:]), ALU.add)
            nc.vector.quantize_mx(out=z_words[:, cols].bitcast(FP8X4), scales=z_scales[:, cols], in_=rounded)

        early, late = slice(0, pieces[-1].start), pieces[-1]
        h_early = [psum.tile([P, early.stop], F32, name="h_early%d" % m, tag="b%d" % m) for m in range(N // P)]
        h_late = [psum.tile([P, PIECE], F32, name="h_late%d" % m, tag="a%d" % m) for m in range(N // P)]

        def h_pass(w_q, z_q, part, start, stop):
            for m in range(N // P):
                cols = slice(m * P, (m + 1) * P)
                nc.tensor.matmul_mx(
                    out=h_late[m][:] if part == late else h_early[m][:, part],
                    lhsT=w_q[0][:, cols].bitcast(FP8X4),
                    lhsT_scale=w_q[1][:, cols],
                    rhs=z_q[0][:, part].bitcast(FP8X4),
                    rhs_scale=z_q[1][:, part],
                    start=start,
                    stop=stop,
                )

        h_pass(w2_q, z2_q, halves[0], True, False)
        h_pass(w2_q, z2_q, slice(HALF, early.stop), False, False)
        h_pass(w2_q, z2_q, late, True, False)
        for part in pieces:
            h_pass(w1_q, (z_words, z_scales), part, False, part.stop >= early.stop)

        h_sbs = [tile([P, S], F32, "h_sb%d" % m) for m in range(N // P)]
        for m in range(EARLY_BANKS_ON_SCALAR):
            nc.scalar.copy(h_sbs[m][:, early], h_early[m][:])
        for m in range(N // P):
            if m >= EARLY_BANKS_ON_SCALAR:
                nc.vector.tensor_copy(h_sbs[m][:, early], h_early[m][:])
            nc.vector.tensor_copy(h_sbs[m][:, late], h_late[m][:])

        for m, h_sb in enumerate(h_sbs):
            h_n7 = tile([P, S], F32, "h_n7_%d" % m)
            diff = tile([P, S], F32, "diff%d" % m)
            res = tile([P, S], F32, "res%d" % m)
            for j, cols in enumerate(halves):
                nc.scalar.activation(h_n7[:, cols], h_sb[:].indirect(entries(l_n7, cols)), ACT.Copy)
                h_at_n6 = h_sb[:].indirect(entries(l_n6, cols))
                if len(halves) * m + j >= FUSED_HALVES:
                    h_n6 = tile([P, HALF], F32, "h_n6_%d%d" % (m, j))
                    nc.scalar.activation(h_n6[:], h_at_n6, ACT.Copy)
                    h_at_n6 = h_n6[:]
                nc.vector.tensor_tensor(diff[:, cols], h_at_n6, h_n7[:, cols], ALU.subtract)
            for cols in halves if m == len(h_sbs) - 1 else [slice(0, S)]:
                nc.vector.tensor_tensor(res[:, cols], diff[:, cols], h_sb[:, cols], ALU.mult)
                nc.sync.dma_start(out[m * P : (m + 1) * P, cols], res[:, cols])
